import numpy as np
import ml_dtypes


def mxq(x, axis, fmt="e4m3"):
    dtype, down = {"e4m3": (ml_dtypes.float8_e4m3fn, 7), "e5m2": (ml_dtypes.float8_e5m2, 14)}[fmt]
    v = np.moveaxis(np.asarray(x, np.float32).astype(ml_dtypes.bfloat16).astype(np.float64), axis, -1)
    blocks = v.reshape(v.shape[:-1] + (-1, 32))
    amax = np.abs(blocks).max(-1, keepdims=True)
    byte = np.maximum(np.where(amax > 0, np.frexp(amax)[1] - 1 + 127, 0) - down, 1)
    scale = np.exp2(byte - 127.0)
    codes = (blocks / scale).astype(np.float32).astype(dtype).astype(np.float64)
    return np.moveaxis((codes * scale).reshape(v.shape), -1, axis)


WIDE = False


def mx_kscale(k):
    if not WIDE:
        return np.ones(k)
    levels = np.array([10, -10, 5, -5, 0])
    if k % 512:
        return np.exp2(np.random.permutation(np.resize(levels, k // 32))).repeat(32)
    a = np.empty((k // 512, 16))
    for p in range(k // 512):
        a[p, :8] = np.random.permutation(np.resize(levels, 8))
        for g in range(8):
            far = levels[np.abs(levels - a[p, g]) >= 10]
            a[p, g + 8] = far[np.random.randint(len(far))]
    return np.exp2(a.ravel()).repeat(32)


def f64(x):
    return np.asarray(x).astype(np.float64)


def striped8(idx):
    return np.asarray(idx).reshape(8, -1, 16).transpose(0, 2, 1).reshape(128, -1).astype(np.uint16)


def unstriped8(offs):
    return offs.reshape(8, 16, -1).transpose(0, 2, 1).reshape(8, -1).astype(np.int64)


def pick8(x, idx, run):
    r = np.arange(len(x))
    return x[r[:, None], idx[r % (8 * run) // run]]


E2M1 = np.array([0.0, 0.5, 1.0, 1.5, 2.0, 3.0, 4.0, 6.0, -0.0, -0.5, -1.0, -1.5, -2.0, -3.0, -4.0, -6.0])


def pack_weight(w, fmt):
    k, n = w.shape
    w = f64(np.asarray(w, np.float32).astype(ml_dtypes.bfloat16)).reshape(k // 32, 32, n)
    amax = np.abs(w).max(1)
    if fmt == "e4m3":
        byte = np.frexp(amax)[1] - 1 + 127 - 7
    else:
        mant, ex = np.frexp(amax / 6.0)
        byte = np.where(mant > 0.5, ex, ex - 1) + 127
    byte = np.clip(np.where(amax > 0, byte, 1), 1, 254)
    scaled = (w * np.exp2(127.0 - byte)[:, None, :]).reshape(k, n).astype(np.float32)
    by_word = np.ascontiguousarray(scaled.reshape(k // 512, 128, 4, n).transpose(0, 1, 3, 2))
    if fmt == "e4m3":
        words = by_word.astype(ml_dtypes.float8_e4m3fn).view(np.uint8)
    else:
        c = by_word.astype(ml_dtypes.float4_e2m1fn).view(np.uint8) & 0xF
        words = (c[..., 0::2] | (c[..., 1::2] << 4)).reshape(k // 512, 128, 2 * n)
    return np.ascontiguousarray(words), np.ascontiguousarray(byte.astype(np.uint8).reshape(k // 512, 16, n))


def unpack_weight(words, scales, fmt):
    g, _, n = scales.shape
    words = np.ascontiguousarray(words).reshape(g, 128, n, -1)
    if fmt == "e4m3":
        vals = words.view(ml_dtypes.float8_e4m3fn).astype(np.float64)
    else:
        nib = np.empty((g, 128, n, 4), np.uint8)
        nib[..., 0::2] = words & 0xF
        nib[..., 1::2] = words >> 4
        vals = E2M1[nib]
    vals = vals * np.repeat(np.exp2(scales.astype(np.float64) - 127.0), 8, axis=1)[..., None]
    return vals.transpose(0, 1, 3, 2).reshape(g * 512, n)


K, J, R, T, U, F, O, D, N, E = 512, 512, 512, 1024, 1024, 1024, 256, 1024, 256, 128


def setup_inputs():
    n = np.random.standard_normal
    idx = np.stack([np.random.permutation(T)[:J] for _ in range(8)])
    idx2 = np.stack([np.random.permutation(U)[:J] for _ in range(8)])
    idx3 = np.stack([np.random.permutation(F)[:R] for _ in range(8)])
    idx4 = np.stack([np.random.permutation(J)[:O] for _ in range(8)])
    idx5 = np.stack([np.random.permutation(D)[:O] for _ in range(8)])
    idx6 = np.stack([np.random.permutation(O)[:E] for _ in range(8)])
    idx7 = np.stack([np.random.permutation(O)[:E] for _ in range(8)])
    fk = mx_kscale(K)
    fr = mx_kscale(R)
    wbp = pack_weight(n((R, N)) * 1 / np.sqrt(R) / fr[:, None], "e4m3")
    wop = pack_weight(n((R, N)) * 1 / np.sqrt(R) / fr[:, None], "e2m1")
    return {
        "ta": (np.random.randint(-7, 8, (K, T)).astype(np.float64)).astype(np.float32),
        "tb": (np.random.randint(1, 9, (K, U)).astype(np.float64)).astype(np.float32),
        "ga": ((np.random.randint(8, 25, (K, 1)) / 64.0) * fk[:, None]).astype(np.float32),
        "gb": (np.random.uniform(0.1, 0.4, (K, 1))).astype(np.float32),
        "ua": (np.random.randint(-7, 8, (K, F)).astype(np.float64)).astype(np.float32),
        "ha": ((np.random.randint(8, 25, (K, 1)) / 1024.0) / fk[:, None]).astype(np.float32),
        "tl": (np.random.randint(-7, 8, (R, D)).astype(np.float64)).astype(np.float32),
        "sa": (np.random.uniform(0.5, 1.6, (R, 1)) * fr[:, None]).astype(np.float32),
        "sl": ((np.random.randint(6, 19, (R, 1)) / 64.0) * fr[:, None]).astype(np.float32),
        "wb_words": wbp[0],
        "wb_scales": wbp[1],
        "wo_words": wop[0],
        "wo_scales": wop[1],
        "so": (np.random.uniform(0.5, 1.6, (N, 1))).astype(np.float32),
        "sp": (np.random.uniform(0.5, 1.6, (N, 1))).astype(np.float32),
        "offs": striped8(idx),
        "offs2": striped8(idx2),
        "offs3": striped8(idx3),
        "offs4": striped8(idx4),
        "offs5": striped8(idx5),
        "offs6": striped8(idx6),
        "offs7": striped8(idx7),
    }


def reference(ta, tb, ga, gb, ua, ha, tl, sa, sl, wb_words, wb_scales, wo_words, wo_scales, so, sp, offs, offs2, offs3, offs4, offs5, offs6, offs7):
    idx = unstriped8(offs)
    idx2 = unstriped8(offs2)
    idx3 = unstriped8(offs3)
    idx4 = unstriped8(offs4)
    idx5 = unstriped8(offs5)
    idx6 = unstriped8(offs6)
    idx7 = unstriped8(offs7)
    wbu = unpack_weight(wb_words, wb_scales, "e4m3")
    wou = unpack_weight(wo_words, wo_scales, "e2m1")
    xc = pick8(f64(ta), idx, 64) * f64(ga) * pick8(f64(tb), idx2, 64) * f64(gb)
    wc = pick8(f64(ua), idx3, 64) * f64(ha)
    wcq = mxq(wc, 0, "e4m3")
    xcq = mxq(xc, 0, "e4m3")
    a = wcq.T @ xcq
    hid = np.maximum(pick8(a, idx4, 64) * f64(sa), pick8(f64(tl), idx5, 64) * f64(sl))
    hidq = mxq(hid, 0, "e4m3")
    p = wbu.T @ hidq
    q = wou.T @ hidq
    y = pick8(p, idx6, 16) * f64(so) - pick8(q, idx7, 16) * f64(sp)
    return y

@@ -1,0 +1,218 @@
+from contextlib import ExitStack
+
+import concourse.mybir as mybir
+
+F32 = mybir.dt.float32
+BF16 = mybir.dt.bfloat16
+I32 = mybir.dt.int32
+U32 = mybir.dt.uint32
+U16 = mybir.dt.uint16
+U8 = mybir.dt.uint8
+FP8X4 = mybir.dt.float8_e4m3fn_x4
+FP4X4 = mybir.dt.float4_e2m1fn_x4
+COPY = mybir.ActivationFunctionType.Copy
+ALU = mybir.AluOpType
+
+P = 128
+PACK = 4
+K, J, R, O, N, E = 512, 512, 512, 256, 256, 128
+TABLE = 1024
+FLOPS = 2 * K * R * J + 2 * 2 * R * N * O
+
+
+def tile_picked_codegain_codes_one_codedlevel_outcomes_outmeet_kernel(
+    tc, ta, tb, ga, gb, ua, ha, tl, sa, sl, wb_words, wb_scales, wo_words, wo_scales, so, sp,
+    offs, offs2, offs3, offs4, offs5, offs6, offs7, out,
+):
+    nc = tc.nc
+    with ExitStack() as ctx:
+        lists = ctx.enter_context(tc.tile_pool(name="lists", bufs=1))
+        sb = ctx.enter_context(tc.tile_pool(name="sb", bufs=1))
+        psum = ctx.enter_context(tc.psum_pool(name="psum", bufs=8))
+
+        def load_list(src, name):
+            tile = lists.tile(list(src.shape), U16, name=name)
+            nc.sync.dma_start(tile[:], src)
+            return tile
+
+        def load_rows(src, t, name):
+            tile = sb.tile([P, TABLE], F32, name=f"{name}{t}", tag=f"{name}{t}")
+            nc.sync.dma_start(tile[:], src.rearrange("(p t) c -> p t c", t=PACK)[:, t, :])
+            return tile
+
+        def load_steps(queue, src, name):
+            tile = sb.tile([P, PACK], F32, name=name)
+            queue.dma_start(tile[:], src.rearrange("(p t) o -> p (t o)", t=PACK))
+            return tile
+
+        def load_out_weights(src, name):
+            tile = sb.tile([P, N // P, 1], F32, name=name)
+            with nc.allow_non_contiguous_dma(reason="one value a partition for each block of 128 output features"):
+                nc.sync.dma_start(tile[:], src.rearrange("(c p) o -> p c o", p=P))
+            return tile
+
+        def load_scale_plane(src, name):
+            staged = sb.tile([4, 4, N // 4], I32, name=f"{name}_staged")
+            nc.gpsimd.dma_start(staged[:], src[0].bitcast(I32).rearrange("(q i) c -> i q c", i=4))
+            plane = sb.tile([P, N], U8, name=name, align_bytes=64)
+            nc.vector.memset(plane[:].bitcast(I32), 0)
+            for q in range(4):
+                nc.vector.tensor_copy(plane[:].bitcast(I32)[32 * q : 32 * q + 4, :], staged[:, q, :])
+            return plane
+
+        def fetch(dst, window, offsets, scale):
+            nc.scalar.activation(out=dst, in_=window[:].indirect(offsets), func=COPY, scale=scale)
+
+        ga_t = load_steps(nc.scalar, ga, "ga_t")
+        gb_t = load_steps(nc.scalar, gb, "gb_t")
+        warm_in = sb.tile([P, 1], F32, name="warm_in")
+        warm_out = sb.tile([P, 1], F32, name="warm_out")
+        nc.vector.memset(warm_in[:], 0.0)
+        nc.scalar.activation(out=warm_out[:], in_=warm_in[:], func=COPY)
+        wb_plane = load_scale_plane(wb_scales, "wb_plane")
+        wo_plane = load_scale_plane(wo_scales, "wo_plane")
+        ha_t = load_steps(nc.gpsimd, ha, "ha_t")
+        sl_t = load_steps(nc.gpsimd, sl, "sl_t")
+        sa_t = load_steps(nc.gpsimd, sa, "sa_t")
+
+        l1 = load_list(offs, "l1")
+        ta_t = [load_rows(ta, 0, "ta")]
+        l2 = load_list(offs2, "l2")
+        tb_t = [load_rows(tb, 0, "tb")]
+        for t in range(1, PACK):
+            ta_t.append(load_rows(ta, t, "ta"))
+            tb_t.append(load_rows(tb, t, "tb"))
+        l3 = load_list(offs3, "l3")
+        ua_t = [load_rows(ua, 0, "ua"), load_rows(ua, 1, "ua")]
+        l5 = load_list(offs5, "l5")
+        ua_t.append(load_rows(ua, 2, "ua"))
+        ua_t.append(load_rows(ua, 3, "ua"))
+        tl_t = [load_rows(tl, t, "tl") for t in range(PACK - 1)]
+        l4 = load_list(offs4, "l4")
+        tl_t.append(load_rows(tl, PACK - 1, "tl"))
+        wb_codes = sb.tile([P, N], U32, name="wb_codes", align_bytes=64)
+        nc.sync.dma_start(wb_codes[:].bitcast(I32), wb_words[0].rearrange("p n t -> p (n t)").bitcast(I32))
+        wo_codes = sb.tile([P, 2 * N], U8, name="wo_codes", align_bytes=64)
+        nc.sync.dma_start(wo_codes[:].bitcast(I32), wo_words[0].bitcast(I32))
+        l6 = load_list(offs6, "l6")
+        l7 = load_list(offs7, "l7")
+        so_t = load_out_weights(so, "so_t")
+        sp_t = load_out_weights(sp, "sp_t")
+
+        code = sb.tile([P, PACK, J], F32, name="code")
+        gain = sb.tile([P, PACK, J], F32, name="gain")
+        xc = sb.tile([P, PACK, J], BF16, name="xc")
+        for t in range(PACK):
+            fetch(code[:, t, :], ta_t[t], l1[:], ga_t[:, t : t + 1])
+            fetch(gain[:, t, :], tb_t[t], l2[:], gb_t[:, t : t + 1])
+            nc.vector.tensor_tensor(xc[:, t, :], code[:, t, :], gain[:, t, :], ALU.mult)
+        xc_woven = sb.tile([P, J, PACK], BF16, name="xc_woven", align_bytes=64)
+        nc.vector.tensor_copy(
+            xc_woven[:].rearrange("p (c i) t -> p c t i", i=4), xc[:].rearrange("p t (c i) -> p c t i", i=4)
+        )
+        xc_codes = sb.tile([P, J], U32, name="xc_codes", align_bytes=64)
+        xc_plane = sb.tile([P, J], U8, name="xc_plane", align_bytes=64)
+        nc.vector.quantize_mx(
+            out=xc_codes[:].bitcast(FP8X4), scales=xc_plane[:], in_=xc_woven[:].rearrange("p j t -> p (j t)")
+        )
+
+        wc = sb.tile([P, PACK, R], BF16, name="wc")
+        wc_woven = sb.tile([P, PACK, P, PACK], BF16, name="wc_woven", align_bytes=64)
+        wc_codes = sb.tile([P, R], U32, name="wc_codes", align_bytes=64)
+        wc_plane = sb.tile([P, R], U8, name="wc_plane", align_bytes=64)
+
+        def weave_wc(pair, m, s):
+            t = slice(2 * pair, 2 * pair + 2)
+            src = wc[:, t, :].rearrange("p t (m s) -> p s m t", s=PACK)[:, s, m, :]
+            nc.vector.tensor_copy(
+                wc_woven[:, s, m, t].rearrange("p s (i e) t -> p i s e t", e=2),
+                src.rearrange("p s (i e) t -> p i s e t", e=2),
+            )
+
+        def quantize_wc(s):
+            cols = slice(s * P, (s + 1) * P)
+            nc.vector.quantize_mx(
+                out=wc_codes[:, cols].bitcast(FP8X4),
+                scales=wc_plane[:, cols],
+                in_=wc_woven[:, s, :, :].rearrange("p m t -> p (m t)"),
+            )
+
+        for t in range(PACK - 1):
+            fetch(wc[:, t, :], ua_t[t], l3[:], ha_t[:, t : t + 1])
+            if t == 1:
+                weave_wc(0, slice(0, P), slice(0, PACK))
+        last = PACK - 1
+        fetch(wc[:, last, : R // 2], ua_t[last], l3[:, :16], ha_t[:, last:])
+        weave_wc(1, slice(0, P // 2), slice(0, PACK))
+        fetch(wc[:, last, R // 2 :], ua_t[last], l3[:, 16:], ha_t[:, last:])
+        for s in range(PACK):
+            weave_wc(1, slice(P // 2, P), slice(s, s + 1))
+            quantize_wc(s)
+
+        level = sb.tile([P, PACK, O], F32, name="level")
+        hid_woven = sb.tile([P, O, PACK], BF16, name="hid_woven", align_bytes=64)
+        hid_codes = sb.tile([P, O], U32, name="hid_codes", align_bytes=64)
+        hid_plane = sb.tile([P, O], U8, name="hid_plane", align_bytes=64)
+        p_t = [sb.tile([P, O], F32, name=f"p{c}") for c in range(N // P)]
+        q_t = [sb.tile([P, O], F32, name=f"q{c}") for c in range(N // P)]
+
+        def product_a(s):
+            a_s = sb.tile([P, J], F32, name=f"a{s}")
+            cols = slice(s * P, (s + 1) * P)
+            for half in range(2):
+                j = slice(half * J // 2, (half + 1) * J // 2)
+                acc = psum.tile([P, J // 2], F32, name="acc", tag="acc")
+                nc.tensor.matmul_mx(
+                    out=acc[:], lhsT=wc_codes[:, cols].bitcast(FP8X4), lhsT_scale=wc_plane[:, cols],
+                    rhs=xc_codes[:, j].bitcast(FP8X4), rhs_scale=xc_plane[:, j], start=True, stop=True,
+                )
+                nc.vector.tensor_copy(a_s[:, j], acc[:])
+            return a_s
+
+        def outcomes(half, hidden):
+            o = slice(half * O // 2, (half + 1) * O // 2)
+            nc.vector.tensor_tensor(
+                hid_woven[:, o, :].rearrange("p (c e) t -> p c t e", e=2),
+                hidden[:].rearrange("p t (c e) -> p c t e", e=2),
+                level[:, :, o].rearrange("p t (c e) -> p c t e", e=2),
+                ALU.max,
+            )
+            nc.vector.quantize_mx(
+                out=hid_codes[:, o].bitcast(FP8X4), scales=hid_plane[:, o],
+                in_=hid_woven[:, o, :].rearrange("p o t -> p (o t)"),
+            )
+            banks = []
+            for c in range(N // P):
+                cols = slice(c * P, (c + 1) * P)
+                for dst, codes, plane in (
+                    (p_t[c], wb_codes[:, cols].bitcast(FP8X4), wb_plane),
+                    (q_t[c], wo_codes[:, 2 * c * P : 2 * (c + 1) * P].bitcast(FP4X4), wo_plane),
+                ):
+                    acc = psum.tile([P, O // 2], F32, name="acc", tag="acc")
+                    nc.tensor.matmul_mx(
+                        out=acc[:], lhsT=codes, lhsT_scale=plane[:, cols],
+                        rhs=hid_codes[:, o].bitcast(FP8X4), rhs_scale=hid_plane[:, o], start=True, stop=True,
+                    )
+                    banks.append((dst[:, o], acc))
+            return banks
+
+        a_t = [product_a(s) for s in range(PACK)]
+        early = sb.tile([P, PACK, O // 2], F32, name="early")
+        for s in range(PACK):
+            fetch(level[:, s, :], tl_t[s], l5[:], sl_t[:, s : s + 1])
+            fetch(early[:, s, :], a_t[s], l4[:, :8], sa_t[:, s : s + 1])
+        banks = outcomes(0, early)
+        late = sb.tile([P, PACK, O // 2], F32, name="late", tag="tl3")
+        for s in range(PACK):
+            fetch(late[:, s, :], a_t[s], l4[:, 8:], sa_t[:, s : s + 1])
+        for dst, acc in banks + outcomes(1, late):
+            nc.vector.tensor_copy(dst, acc[:])
+
+        for c in range(N // P):
+            first = sb.tile([P, E], F32, name=f"first{c}")
+            second = sb.tile([P, E], F32, name=f"second{c}")
+            y = sb.tile([P, E], F32, name=f"y{c}")
+            fetch(first[:], p_t[c], l6[:], so_t[:, c, :])
+            fetch(second[:], q_t[c], l7[:], sp_t[:, c, :])
+            nc.vector.tensor_tensor(y[:], first[:], second[:], ALU.subtract)
+            nc.sync.dma_start(out[c * P : (c + 1) * P, :], y[:])

@@ -40,9 +40,9 @@ def tile_picked_codegain_codes_one_codedlevel_outcomes_outmeet_kernel(
             nc.sync.dma_start(tile[:], src.rearrange("(p t) c -> p t c", t=PACK)[:, t, :])
             return tile
 
-        def load_steps(queue, src, name):
-            tile = sb.tile([P, PACK], F32, name=name)
-            queue.dma_start(tile[:], src.rearrange("(p t) o -> p (t o)", t=PACK))
+        def load_steps(queue, src, name, t0=0, t1=PACK):
+            tile = sb.tile([P, t1 - t0], F32, name=name)
+            queue.dma_start(tile[:], src.rearrange("(p t) o -> p (t o)", t=PACK)[:, t0:t1])
             return tile
 
         def load_out_weights(src, name):
@@ -51,49 +51,54 @@ def tile_picked_codegain_codes_one_codedlevel_outcomes_outmeet_kernel(
                 nc.sync.dma_start(tile[:], src.rearrange("(c p) o -> p c o", p=P))
             return tile
 
-        def load_scale_plane(src, name):
-            staged = sb.tile([4, 4, N // 4], I32, name=f"{name}_staged")
-            nc.gpsimd.dma_start(staged[:], src[0].bitcast(I32).rearrange("(q i) c -> i q c", i=4))
+        def new_scale_plane(name):
             plane = sb.tile([P, N], U8, name=name, align_bytes=64)
             nc.vector.memset(plane[:].bitcast(I32), 0)
-            for q in range(4):
-                nc.vector.tensor_copy(plane[:].bitcast(I32)[32 * q : 32 * q + 4, :], staged[:, q, :])
             return plane
+
+        def load_scale_rows(plane, src, q):
+            nc.sync.dma_start(
+                plane[:].bitcast(I32)[32 * q : 32 * q + 4, :], src[0].bitcast(I32)[4 * q : 4 * q + 4, :]
+            )
 
         def fetch(dst, window, offsets, scale):
             nc.scalar.activation(out=dst, in_=window[:].indirect(offsets), func=COPY, scale=scale)
 
         ga_t = load_steps(nc.scalar, ga, "ga_t")
-        gb_t = load_steps(nc.scalar, gb, "gb_t")
         warm_in = sb.tile([P, 1], F32, name="warm_in")
         warm_out = sb.tile([P, 1], F32, name="warm_out")
         nc.vector.memset(warm_in[:], 0.0)
         nc.scalar.activation(out=warm_out[:], in_=warm_in[:], func=COPY)
-        wb_plane = load_scale_plane(wb_scales, "wb_plane")
-        wo_plane = load_scale_plane(wo_scales, "wo_plane")
-        ha_t = load_steps(nc.gpsimd, ha, "ha_t")
-        sl_t = load_steps(nc.gpsimd, sl, "sl_t")
-        sa_t = load_steps(nc.gpsimd, sa, "sa_t")
 
-        l1 = load_list(offs, "l1")
-        ta_t = [load_rows(ta, 0, "ta")]
-        l2 = load_list(offs2, "l2")
-        tb_t = [load_rows(tb, 0, "tb")]
-        for t in range(1, PACK):
+        wb_plane = new_scale_plane("wb_plane")
+        wo_plane = new_scale_plane("wo_plane")
+        ta_t, tb_t = [], []
+        for t in range(PACK):
             ta_t.append(load_rows(ta, t, "ta"))
+            if t == 0:
+                l1 = load_list(offs, "l1")
+                l2 = load_list(offs2, "l2")
+                gb_t = load_steps(nc.sync, gb, "gb_t")
             tb_t.append(load_rows(tb, t, "tb"))
         l3 = load_list(offs3, "l3")
-        ua_t = [load_rows(ua, 0, "ua"), load_rows(ua, 1, "ua")]
+        ha_t = load_steps(nc.sync, ha, "ha_t")
+        ua_t = [load_rows(ua, t, "ua") for t in range(PACK)]
         l5 = load_list(offs5, "l5")
-        ua_t.append(load_rows(ua, 2, "ua"))
-        ua_t.append(load_rows(ua, 3, "ua"))
+        sl_t = load_steps(nc.sync, sl, "sl_t")
         tl_t = [load_rows(tl, t, "tl") for t in range(PACK - 1)]
         l4 = load_list(offs4, "l4")
+        sa_lo = load_steps(nc.sync, sa, "sa_lo", 0, 2)
         tl_t.append(load_rows(tl, PACK - 1, "tl"))
+        sa_hi = load_steps(nc.sync, sa, "sa_hi", 2, 4)
+        sa_t = [sa_lo[:, 0:1], sa_lo[:, 1:2], sa_hi[:, 0:1], sa_hi[:, 1:2]]
         wb_codes = sb.tile([P, N], U32, name="wb_codes", align_bytes=64)
         nc.sync.dma_start(wb_codes[:].bitcast(I32), wb_words[0].rearrange("p n t -> p (n t)").bitcast(I32))
+        for q in range(4):
+            load_scale_rows(wb_plane, wb_scales, q)
         wo_codes = sb.tile([P, 2 * N], U8, name="wo_codes", align_bytes=64)
         nc.sync.dma_start(wo_codes[:].bitcast(I32), wo_words[0].bitcast(I32))
+        for q in range(4):
+            load_scale_rows(wo_plane, wo_scales, q)
         l6 = load_list(offs6, "l6")
         l7 = load_list(offs7, "l7")
         so_t = load_out_weights(so, "so_t")
@@ -150,7 +155,6 @@ def tile_picked_codegain_codes_one_codedlevel_outcomes_outmeet_kernel(
             quantize_wc(s)
 
         level = sb.tile([P, PACK, O], F32, name="level")
-        hid_woven = sb.tile([P, O, PACK], BF16, name="hid_woven", align_bytes=64)
         hid_codes = sb.tile([P, O], U32, name="hid_codes", align_bytes=64)
         hid_plane = sb.tile([P, O], U8, name="hid_plane", align_bytes=64)
         p_t = [sb.tile([P, O], F32, name=f"p{c}") for c in range(N // P)]
@@ -171,16 +175,20 @@ def tile_picked_codegain_codes_one_codedlevel_outcomes_outmeet_kernel(
 
         def outcomes(half, hidden):
             o = slice(half * O // 2, (half + 1) * O // 2)
-            nc.vector.tensor_tensor(
-                hid_woven[:, o, :].rearrange("p (c e) t -> p c t e", e=2),
-                hidden[:].rearrange("p t (c e) -> p c t e", e=2),
-                level[:, :, o].rearrange("p t (c e) -> p c t e", e=2),
-                ALU.max,
-            )
-            nc.vector.quantize_mx(
-                out=hid_codes[:, o].bitcast(FP8X4), scales=hid_plane[:, o],
-                in_=hid_woven[:, o, :].rearrange("p o t -> p (o t)"),
-            )
+            hid_woven = sb.tile([P, O // 2, PACK], BF16, name="hid_woven", tag="hid_woven", align_bytes=64)
+            pieces = [slice(u * O // 4, (u + 1) * O // 4) for u in range(2)]
+            for u in pieces:
+                nc.vector.tensor_tensor(
+                    hid_woven[:, u, :].rearrange("p (c e) t -> p c t e", e=2),
+                    hidden[:, :, u].rearrange("p t (c e) -> p c t e", e=2),
+                    level[:, :, o][:, :, u].rearrange("p t (c e) -> p c t e", e=2),
+                    ALU.max,
+                )
+            for u in pieces:
+                nc.vector.quantize_mx(
+                    out=hid_codes[:, o][:, u].bitcast(FP8X4), scales=hid_plane[:, o][:, u],
+                    in_=hid_woven[:, u, :].rearrange("p o t -> p (o t)"),
+                )
             banks = []
             for c in range(N // P):
                 cols = slice(c * P, (c + 1) * P)
@@ -200,11 +208,11 @@ def tile_picked_codegain_codes_one_codedlevel_outcomes_outmeet_kernel(
         early = sb.tile([P, PACK, O // 2], F32, name="early")
         for s in range(PACK):
             fetch(level[:, s, :], tl_t[s], l5[:], sl_t[:, s : s + 1])
-            fetch(early[:, s, :], a_t[s], l4[:, :8], sa_t[:, s : s + 1])
+            fetch(early[:, s, :], a_t[s], l4[:, :8], sa_t[s])
         banks = outcomes(0, early)
         late = sb.tile([P, PACK, O // 2], F32, name="late", tag="tl3")
         for s in range(PACK):
-            fetch(late[:, s, :], a_t[s], l4[:, 8:], sa_t[:, s : s + 1])
+            fetch(late[:, s, :], a_t[s], l4[:, 8:], sa_t[s])
         for dst, acc in banks + outcomes(1, late):
             nc.vector.tensor_copy(dst, acc[:])
 

@@ -14,10 +14,19 @@ COPY = mybir.ActivationFunctionType.Copy
 ALU = mybir.AluOpType
 
 P = 128
-PACK = 4
+PLANES = 4
+LAST = PLANES - 1
 K, J, R, O, N, E = 512, 512, 512, 256, 256, 128
 TABLE = 1024
+BLOCKS = N // P
+QUADRANTS = 4
+PER_COLUMN = 16
+PSUM_BANKS = 8
 FLOPS = 2 * K * R * J + 2 * 2 * R * N * O
+
+
+def halves(n):
+    return slice(0, n // 2), slice(n // 2, n)
 
 
 def tile_picked_codegain_codes_one_codedlevel_outcomes_outmeet_kernel(
@@ -28,199 +37,193 @@ def tile_picked_codegain_codes_one_codedlevel_outcomes_outmeet_kernel(
     with ExitStack() as ctx:
         lists = ctx.enter_context(tc.tile_pool(name="lists", bufs=1))
         sb = ctx.enter_context(tc.tile_pool(name="sb", bufs=1))
-        psum = ctx.enter_context(tc.psum_pool(name="psum", bufs=8))
+        psum = ctx.enter_context(tc.psum_pool(name="psum", bufs=PSUM_BANKS))
 
         def load_list(src, name):
             tile = lists.tile(list(src.shape), U16, name=name)
             nc.sync.dma_start(tile[:], src)
             return tile
 
-        def load_rows(src, t, name):
-            tile = sb.tile([P, TABLE], F32, name=f"{name}{t}", tag=f"{name}{t}")
-            nc.sync.dma_start(tile[:], src.rearrange("(p t) c -> p t c", t=PACK)[:, t, :])
+        def load_plane(src, t, name):
+            tile = sb.tile([P, TABLE], F32, name=f"{name}{t}")
+            nc.sync.dma_start(tile[:], src.rearrange("(p t) c -> p t c", t=PLANES)[:, t, :])
             return tile
 
-        def load_steps(queue, src, name, t0=0, t1=PACK):
+        def load_factors(queue, src, name, t0=0, t1=PLANES):
             tile = sb.tile([P, t1 - t0], F32, name=name)
-            queue.dma_start(tile[:], src.rearrange("(p t) o -> p (t o)", t=PACK)[:, t0:t1])
-            return tile
+            with nc.allow_non_contiguous_dma(reason="up to four values a partition"):
+                queue.dma_start(tile[:], src.rearrange("(p t) o -> p (t o)", t=PLANES)[:, t0:t1])
+            return [tile[:, t : t + 1] for t in range(t1 - t0)]
 
-        def load_out_weights(src, name):
-            tile = sb.tile([P, N // P, 1], F32, name=name)
-            with nc.allow_non_contiguous_dma(reason="one value a partition for each block of 128 output features"):
+        def load_output_factors(src, name):
+            tile = sb.tile([P, BLOCKS, 1], F32, name=name)
+            with nc.allow_non_contiguous_dma(reason="one value a partition for each block of output features"):
                 nc.sync.dma_start(tile[:], src.rearrange("(c p) o -> p c o", p=P))
+            return [tile[:, c, :] for c in range(BLOCKS)]
+
+        def new_scale_tile(name):
+            tile = sb.tile([P, N], U8, name=name, align_bytes=64)
+            nc.vector.memset(tile[:].bitcast(I32), 0)
             return tile
 
-        def new_scale_plane(name):
-            plane = sb.tile([P, N], U8, name=name, align_bytes=64)
-            nc.vector.memset(plane[:].bitcast(I32), 0)
-            return plane
+        def load_scale_rows(tile, src):
+            for u in range(QUADRANTS):
+                nc.sync.dma_start(
+                    tile[:].bitcast(I32)[32 * u : 32 * u + 4, :], src[0].bitcast(I32)[4 * u : 4 * u + 4, :]
+                )
 
-        def load_scale_rows(plane, src, q):
-            nc.sync.dma_start(
-                plane[:].bitcast(I32)[32 * q : 32 * q + 4, :], src[0].bitcast(I32)[4 * q : 4 * q + 4, :]
-            )
-
-        def fetch(dst, window, offsets, scale):
+        def fetch(dst, window, list_tile, scale, entries=None):
+            if entries is None:
+                offsets = list_tile[:]
+            else:
+                offsets = list_tile[:, entries.start // PER_COLUMN : entries.stop // PER_COLUMN]
             nc.scalar.activation(out=dst, in_=window[:].indirect(offsets), func=COPY, scale=scale)
 
-        ga_t = load_steps(nc.scalar, ga, "ga_t")
+        def quantize(codes, scales, woven):
+            nc.vector.quantize_mx(out=codes.bitcast(FP8X4), scales=scales, in_=woven.rearrange("p c t -> p (c t)"))
+
+        def product(lhsT, lhsT_scale, rhs, rhs_scale):
+            acc = psum.tile([P, rhs.shape[1]], F32, name="acc", tag="acc")
+            nc.tensor.matmul_mx(
+                out=acc[:], lhsT=lhsT, lhsT_scale=lhsT_scale, rhs=rhs.bitcast(FP8X4), rhs_scale=rhs_scale,
+                start=True, stop=True,
+            )
+            return acc
+
+        ga_f = load_factors(nc.scalar, ga, "ga_f")
         warm_in = sb.tile([P, 1], F32, name="warm_in")
         warm_out = sb.tile([P, 1], F32, name="warm_out")
         nc.vector.memset(warm_in[:], 0.0)
         nc.scalar.activation(out=warm_out[:], in_=warm_in[:], func=COPY)
 
-        wb_plane = new_scale_plane("wb_plane")
-        wo_plane = new_scale_plane("wo_plane")
-        ta_t, tb_t = [], []
-        for t in range(PACK):
-            ta_t.append(load_rows(ta, t, "ta"))
-            if t == 0:
-                l1 = load_list(offs, "l1")
-                l2 = load_list(offs2, "l2")
-                gb_t = load_steps(nc.sync, gb, "gb_t")
-            tb_t.append(load_rows(tb, t, "tb"))
-        l3 = load_list(offs3, "l3")
-        ha_t = load_steps(nc.sync, ha, "ha_t")
-        ua_t = [load_rows(ua, t, "ua") for t in range(PACK)]
-        l5 = load_list(offs5, "l5")
-        sl_t = load_steps(nc.sync, sl, "sl_t")
-        tl_t = [load_rows(tl, t, "tl") for t in range(PACK - 1)]
-        l4 = load_list(offs4, "l4")
-        sa_lo = load_steps(nc.sync, sa, "sa_lo", 0, 2)
-        tl_t.append(load_rows(tl, PACK - 1, "tl"))
-        sa_hi = load_steps(nc.sync, sa, "sa_hi", 2, 4)
-        sa_t = [sa_lo[:, 0:1], sa_lo[:, 1:2], sa_hi[:, 0:1], sa_hi[:, 1:2]]
+        wb_scale = new_scale_tile("wb_scale")
+        wo_scale = new_scale_tile("wo_scale")
+        ta_p = [load_plane(ta, 0, "ta")]
+        list1 = load_list(offs, "list1")
+        list2 = load_list(offs2, "list2")
+        gb_f = load_factors(nc.sync, gb, "gb_f")
+        tb_p = [load_plane(tb, 0, "tb")]
+        for t in range(1, PLANES):
+            ta_p.append(load_plane(ta, t, "ta"))
+            tb_p.append(load_plane(tb, t, "tb"))
+        list3 = load_list(offs3, "list3")
+        ha_f = load_factors(nc.sync, ha, "ha_f")
+        ua_p = [load_plane(ua, t, "ua") for t in range(PLANES)]
+        list5 = load_list(offs5, "list5")
+        sl_f = load_factors(nc.sync, sl, "sl_f")
+        tl_p = [load_plane(tl, t, "tl") for t in range(LAST)]
+        list4 = load_list(offs4, "list4")
+        sa_f = load_factors(nc.sync, sa, "sa_first", 0, 1)
+        tl_p.append(load_plane(tl, LAST, "tl"))
+        sa_f = sa_f + load_factors(nc.sync, sa, "sa_rest", 1, PLANES)
         wb_codes = sb.tile([P, N], U32, name="wb_codes", align_bytes=64)
         nc.sync.dma_start(wb_codes[:].bitcast(I32), wb_words[0].rearrange("p n t -> p (n t)").bitcast(I32))
-        for q in range(4):
-            load_scale_rows(wb_plane, wb_scales, q)
+        load_scale_rows(wb_scale, wb_scales)
         wo_codes = sb.tile([P, 2 * N], U8, name="wo_codes", align_bytes=64)
         nc.sync.dma_start(wo_codes[:].bitcast(I32), wo_words[0].bitcast(I32))
-        for q in range(4):
-            load_scale_rows(wo_plane, wo_scales, q)
-        l6 = load_list(offs6, "l6")
-        l7 = load_list(offs7, "l7")
-        so_t = load_out_weights(so, "so_t")
-        sp_t = load_out_weights(sp, "sp_t")
+        load_scale_rows(wo_scale, wo_scales)
+        list6 = load_list(offs6, "list6")
+        list7 = load_list(offs7, "list7")
+        so_f = load_output_factors(so, "so_f")
+        sp_f = load_output_factors(sp, "sp_f")
 
-        code = sb.tile([P, PACK, J], F32, name="code")
-        gain = sb.tile([P, PACK, J], F32, name="gain")
-        xc = sb.tile([P, PACK, J], BF16, name="xc")
-        for t in range(PACK):
-            fetch(code[:, t, :], ta_t[t], l1[:], ga_t[:, t : t + 1])
-            fetch(gain[:, t, :], tb_t[t], l2[:], gb_t[:, t : t + 1])
+        code = sb.tile([P, PLANES, J], F32, name="code")
+        gain = sb.tile([P, PLANES, J], F32, name="gain")
+        xc = sb.tile([P, PLANES, J], BF16, name="xc")
+        for t in range(PLANES):
+            fetch(code[:, t, :], ta_p[t], list1, ga_f[t])
+            fetch(gain[:, t, :], tb_p[t], list2, gb_f[t])
             nc.vector.tensor_tensor(xc[:, t, :], code[:, t, :], gain[:, t, :], ALU.mult)
-        xc_woven = sb.tile([P, J, PACK], BF16, name="xc_woven", align_bytes=64)
+        xc_woven = sb.tile([P, J, PLANES], BF16, name="xc_woven", align_bytes=64)
         nc.vector.tensor_copy(
             xc_woven[:].rearrange("p (c i) t -> p c t i", i=4), xc[:].rearrange("p t (c i) -> p c t i", i=4)
         )
         xc_codes = sb.tile([P, J], U32, name="xc_codes", align_bytes=64)
-        xc_plane = sb.tile([P, J], U8, name="xc_plane", align_bytes=64)
-        nc.vector.quantize_mx(
-            out=xc_codes[:].bitcast(FP8X4), scales=xc_plane[:], in_=xc_woven[:].rearrange("p j t -> p (j t)")
-        )
+        xc_scale = sb.tile([P, J], U8, name="xc_scale", align_bytes=64)
+        quantize(xc_codes[:], xc_scale[:], xc_woven[:])
 
-        wc = sb.tile([P, PACK, R], BF16, name="wc")
-        wc_woven = sb.tile([P, PACK, P, PACK], BF16, name="wc_woven", align_bytes=64)
+        wc = sb.tile([P, PLANES, R], BF16, name="wc")
+        wc_woven = sb.tile([P, PLANES, P, PLANES], BF16, name="wc_woven", align_bytes=64)
         wc_codes = sb.tile([P, R], U32, name="wc_codes", align_bytes=64)
-        wc_plane = sb.tile([P, R], U8, name="wc_plane", align_bytes=64)
+        wc_scale = sb.tile([P, R], U8, name="wc_scale", align_bytes=64)
 
-        def weave_wc(pair, m, s):
-            t = slice(2 * pair, 2 * pair + 2)
-            src = wc[:, t, :].rearrange("p t (m s) -> p s m t", s=PACK)[:, s, m, :]
+        def weave_wc(t, m, s):
+            src = wc[:, t, :].rearrange("p t (m s) -> p s m t", s=PLANES)[:, s, m, :]
             nc.vector.tensor_copy(
                 wc_woven[:, s, m, t].rearrange("p s (i e) t -> p i s e t", e=2),
                 src.rearrange("p s (i e) t -> p i s e t", e=2),
             )
 
-        def quantize_wc(s):
+        low_planes, high_planes = halves(PLANES)
+        low_m, high_m = halves(P)
+        low_r, high_r = halves(R)
+        all_groups = slice(0, PLANES)
+        for t in range(low_planes.stop):
+            fetch(wc[:, t, :], ua_p[t], list3, ha_f[t])
+        weave_wc(low_planes, slice(0, P), all_groups)
+        fetch(wc[:, LAST - 1, :], ua_p[LAST - 1], list3, ha_f[LAST - 1])
+        fetch(wc[:, LAST, low_r], ua_p[LAST], list3, ha_f[LAST], low_r)
+        weave_wc(high_planes, low_m, all_groups)
+        fetch(wc[:, LAST, high_r], ua_p[LAST], list3, ha_f[LAST], high_r)
+        for s in range(PLANES):
+            weave_wc(high_planes, high_m, slice(s, s + 1))
             cols = slice(s * P, (s + 1) * P)
-            nc.vector.quantize_mx(
-                out=wc_codes[:, cols].bitcast(FP8X4),
-                scales=wc_plane[:, cols],
-                in_=wc_woven[:, s, :, :].rearrange("p m t -> p (m t)"),
-            )
+            quantize(wc_codes[:, cols], wc_scale[:, cols], wc_woven[:, s, :, :])
 
-        for t in range(PACK - 1):
-            fetch(wc[:, t, :], ua_t[t], l3[:], ha_t[:, t : t + 1])
-            if t == 1:
-                weave_wc(0, slice(0, P), slice(0, PACK))
-        last = PACK - 1
-        fetch(wc[:, last, : R // 2], ua_t[last], l3[:, :16], ha_t[:, last:])
-        weave_wc(1, slice(0, P // 2), slice(0, PACK))
-        fetch(wc[:, last, R // 2 :], ua_t[last], l3[:, 16:], ha_t[:, last:])
-        for s in range(PACK):
-            weave_wc(1, slice(P // 2, P), slice(s, s + 1))
-            quantize_wc(s)
-
-        level = sb.tile([P, PACK, O], F32, name="level")
+        level = sb.tile([P, PLANES, O], F32, name="level")
         hid_codes = sb.tile([P, O], U32, name="hid_codes", align_bytes=64)
-        hid_plane = sb.tile([P, O], U8, name="hid_plane", align_bytes=64)
-        p_t = [sb.tile([P, O], F32, name=f"p{c}") for c in range(N // P)]
-        q_t = [sb.tile([P, O], F32, name=f"q{c}") for c in range(N // P)]
-
-        def product_a(s):
-            a_s = sb.tile([P, J], F32, name=f"a{s}")
+        hid_scale = sb.tile([P, O], U8, name="hid_scale", align_bytes=64)
+        p_b = [sb.tile([P, O], F32, name=f"p{c}") for c in range(BLOCKS)]
+        q_b = [sb.tile([P, O], F32, name=f"q{c}") for c in range(BLOCKS)]
+        a_p = []
+        for s in range(PLANES):
+            a_p.append(sb.tile([P, J], F32, name=f"a{s}"))
             cols = slice(s * P, (s + 1) * P)
-            for half in range(2):
-                j = slice(half * J // 2, (half + 1) * J // 2)
-                acc = psum.tile([P, J // 2], F32, name="acc", tag="acc")
-                nc.tensor.matmul_mx(
-                    out=acc[:], lhsT=wc_codes[:, cols].bitcast(FP8X4), lhsT_scale=wc_plane[:, cols],
-                    rhs=xc_codes[:, j].bitcast(FP8X4), rhs_scale=xc_plane[:, j], start=True, stop=True,
-                )
-                nc.vector.tensor_copy(a_s[:, j], acc[:])
-            return a_s
+            width = J // 4 if s == 0 else J // 2
+            for j0 in range(0, J, width):
+                j = slice(j0, j0 + width)
+                acc = product(wc_codes[:, cols].bitcast(FP8X4), wc_scale[:, cols], xc_codes[:, j], xc_scale[:, j])
+                nc.vector.tensor_copy(a_p[s][:, j], acc[:])
 
-        def outcomes(half, hidden):
-            o = slice(half * O // 2, (half + 1) * O // 2)
-            hid_woven = sb.tile([P, O // 2, PACK], BF16, name="hid_woven", tag="hid_woven", align_bytes=64)
-            pieces = [slice(u * O // 4, (u + 1) * O // 4) for u in range(2)]
-            for u in pieces:
+        hidden = sb.tile([P, PLANES, O], F32, name="hidden")
+
+        def outcomes(o):
+            hid_woven = sb.tile([P, O // 2, PLANES], BF16, name="hid_woven", tag="hid_woven", align_bytes=64)
+            for piece in halves(O // 2):
                 nc.vector.tensor_tensor(
-                    hid_woven[:, u, :].rearrange("p (c e) t -> p c t e", e=2),
-                    hidden[:, :, u].rearrange("p t (c e) -> p c t e", e=2),
-                    level[:, :, o][:, :, u].rearrange("p t (c e) -> p c t e", e=2),
+                    hid_woven[:, piece, :].rearrange("p (c e) t -> p c t e", e=2),
+                    hidden[:, :, o][:, :, piece].rearrange("p t (c e) -> p c t e", e=2),
+                    level[:, :, o][:, :, piece].rearrange("p t (c e) -> p c t e", e=2),
                     ALU.max,
                 )
-            for u in pieces:
-                nc.vector.quantize_mx(
-                    out=hid_codes[:, o][:, u].bitcast(FP8X4), scales=hid_plane[:, o][:, u],
-                    in_=hid_woven[:, u, :].rearrange("p o t -> p (o t)"),
-                )
+            for piece in halves(O // 2):
+                quantize(hid_codes[:, o][:, piece], hid_scale[:, o][:, piece], hid_woven[:, piece, :])
             banks = []
-            for c in range(N // P):
+            for c in range(BLOCKS):
                 cols = slice(c * P, (c + 1) * P)
-                for dst, codes, plane in (
-                    (p_t[c], wb_codes[:, cols].bitcast(FP8X4), wb_plane),
-                    (q_t[c], wo_codes[:, 2 * c * P : 2 * (c + 1) * P].bitcast(FP4X4), wo_plane),
-                ):
-                    acc = psum.tile([P, O // 2], F32, name="acc", tag="acc")
-                    nc.tensor.matmul_mx(
-                        out=acc[:], lhsT=codes, lhsT_scale=plane[:, cols],
-                        rhs=hid_codes[:, o].bitcast(FP8X4), rhs_scale=hid_plane[:, o], start=True, stop=True,
-                    )
-                    banks.append((dst[:, o], acc))
+                wb_block = wb_codes[:, cols].bitcast(FP8X4)
+                wo_block = wo_codes[:, 2 * c * P : 2 * (c + 1) * P].bitcast(FP4X4)
+                banks.append((p_b[c][:, o], product(wb_block, wb_scale[:, cols], hid_codes[:, o], hid_scale[:, o])))
+                banks.append((q_b[c][:, o], product(wo_block, wo_scale[:, cols], hid_codes[:, o], hid_scale[:, o])))
             return banks
 
-        a_t = [product_a(s) for s in range(PACK)]
-        early = sb.tile([P, PACK, O // 2], F32, name="early")
-        for s in range(PACK):
-            fetch(level[:, s, :], tl_t[s], l5[:], sl_t[:, s : s + 1])
-            fetch(early[:, s, :], a_t[s], l4[:, :8], sa_t[s])
-        banks = outcomes(0, early)
-        late = sb.tile([P, PACK, O // 2], F32, name="late", tag="tl3")
-        for s in range(PACK):
-            fetch(late[:, s, :], a_t[s], l4[:, 8:], sa_t[s])
-        for dst, acc in banks + outcomes(1, late):
+        low_o, high_o = halves(O)
+        for s in range(PLANES):
+            fetch(level[:, s, :], tl_p[s], list5, sl_f[s])
+        fetch(hidden[:, 0, :], a_p[0], list4, sa_f[0])
+        for s in range(1, PLANES):
+            fetch(hidden[:, s, low_o], a_p[s], list4, sa_f[s], low_o)
+        banks = outcomes(low_o)
+        for s in range(1, PLANES):
+            fetch(hidden[:, s, high_o], a_p[s], list4, sa_f[s], high_o)
+        for dst, acc in banks + outcomes(high_o):
             nc.vector.tensor_copy(dst, acc[:])
 
-        for c in range(N // P):
+        for c in range(BLOCKS):
             first = sb.tile([P, E], F32, name=f"first{c}")
             second = sb.tile([P, E], F32, name=f"second{c}")
             y = sb.tile([P, E], F32, name=f"y{c}")
-            fetch(first[:], p_t[c], l6[:], so_t[:, c, :])
-            fetch(second[:], q_t[c], l7[:], sp_t[:, c, :])
+            fetch(first[:], p_b[c], list6, so_f[c])
+            fetch(second[:], q_b[c], list7, sp_f[c])
             nc.vector.tensor_tensor(y[:], first[:], second[:], ALU.subtract)
             nc.sync.dma_start(out[c * P : (c + 1) * P, :], y[:])

from contextlib import ExitStack

import concourse.mybir as mybir

F32 = mybir.dt.float32
BF16 = mybir.dt.bfloat16
I32 = mybir.dt.int32
U32 = mybir.dt.uint32
U16 = mybir.dt.uint16
U8 = mybir.dt.uint8
FP8X4 = mybir.dt.float8_e4m3fn_x4
FP4X4 = mybir.dt.float4_e2m1fn_x4
COPY = mybir.ActivationFunctionType.Copy
ALU = mybir.AluOpType

P = 128
PLANES = 4
LAST = PLANES - 1
K, J, R, O, N, E = 512, 512, 512, 256, 256, 128
TABLE = 1024
BLOCKS = N // P
QUADRANTS = 4
PER_COLUMN = 16
PSUM_BANKS = 8
FLOPS = 2 * K * R * J + 2 * 2 * R * N * O


def halves(n):
    return slice(0, n // 2), slice(n // 2, n)


def tile_picked_codegain_codes_one_codedlevel_outcomes_outmeet_kernel(
    tc, ta, tb, ga, gb, ua, ha, tl, sa, sl, wb_words, wb_scales, wo_words, wo_scales, so, sp,
    offs, offs2, offs3, offs4, offs5, offs6, offs7, out,
):
    nc = tc.nc
    with ExitStack() as ctx:
        lists = ctx.enter_context(tc.tile_pool(name="lists", bufs=1))
        sb = ctx.enter_context(tc.tile_pool(name="sb", bufs=1))
        psum = ctx.enter_context(tc.psum_pool(name="psum", bufs=PSUM_BANKS))

        def load_list(src, name):
            tile = lists.tile(list(src.shape), U16, name=name)
            nc.sync.dma_start(tile[:], src)
            return tile

        def load_plane(src, t, name):
            tile = sb.tile([P, TABLE], F32, name=f"{name}{t}")
            nc.sync.dma_start(tile[:], src.rearrange("(p t) c -> p t c", t=PLANES)[:, t, :])
            return tile

        def load_factors(queue, src, name, t0=0, t1=PLANES):
            tile = sb.tile([P, t1 - t0], F32, name=name)
            with nc.allow_non_contiguous_dma(reason="up to four values a partition"):
                queue.dma_start(tile[:], src.rearrange("(p t) o -> p (t o)", t=PLANES)[:, t0:t1])
            return [tile[:, t : t + 1] for t in range(t1 - t0)]

        def load_output_factors(src, name):
            tile = sb.tile([P, BLOCKS, 1], F32, name=name)
            with nc.allow_non_contiguous_dma(reason="one value a partition for each block of output features"):
                nc.sync.dma_start(tile[:], src.rearrange("(c p) o -> p c o", p=P))
            return [tile[:, c, :] for c in range(BLOCKS)]

        def new_scale_tile(name):
            tile = sb.tile([P, N], U8, name=name, align_bytes=64)
            nc.vector.memset(tile[:].bitcast(I32), 0)
            return tile

        def load_scale_rows(tile, src):
            for u in range(QUADRANTS):
                nc.sync.dma_start(
                    tile[:].bitcast(I32)[32 * u : 32 * u + 4, :], src[0].bitcast(I32)[4 * u : 4 * u + 4, :]
                )

        def fetch(dst, window, list_tile, scale, entries=None):
            if entries is None:
                offsets = list_tile[:]
            else:
                offsets = list_tile[:, entries.start // PER_COLUMN : entries.stop // PER_COLUMN]
            nc.scalar.activation(out=dst, in_=window[:].indirect(offsets), func=COPY, scale=scale)

        def quantize(codes, scales, woven):
            nc.vector.quantize_mx(out=codes.bitcast(FP8X4), scales=scales, in_=woven.rearrange("p c t -> p (c t)"))

        def product(lhsT, lhsT_scale, rhs, rhs_scale):
            acc = psum.tile([P, rhs.shape[1]], F32, name="acc", tag="acc")
            nc.tensor.matmul_mx(
                out=acc[:], lhsT=lhsT, lhsT_scale=lhsT_scale, rhs=rhs.bitcast(FP8X4), rhs_scale=rhs_scale,
                start=True, stop=True,
            )
            return acc

        ga_f = load_factors(nc.scalar, ga, "ga_f")
        warm_in = sb.tile([P, 1], F32, name="warm_in")
        warm_out = sb.tile([P, 1], F32, name="warm_out")
        nc.vector.memset(warm_in[:], 0.0)
        nc.scalar.activation(out=warm_out[:], in_=warm_in[:], func=COPY)

        wb_scale = new_scale_tile("wb_scale")
        wo_scale = new_scale_tile("wo_scale")
        ta_p = [load_plane(ta, 0, "ta")]
        list1 = load_list(offs, "list1")
        list2 = load_list(offs2, "list2")
        gb_f = load_factors(nc.sync, gb, "gb_f")
        tb_p = [load_plane(tb, 0, "tb")]
        for t in range(1, PLANES):
            ta_p.append(load_plane(ta, t, "ta"))
            tb_p.append(load_plane(tb, t, "tb"))
        list3 = load_list(offs3, "list3")
        ha_f = load_factors(nc.sync, ha, "ha_f")
        ua_p = [load_plane(ua, t, "ua") for t in range(PLANES)]
        list5 = load_list(offs5, "list5")
        sl_f = load_factors(nc.sync, sl, "sl_f")
        tl_p = [load_plane(tl, t, "tl") for t in range(LAST)]
        list4 = load_list(offs4, "list4")
        sa_f = load_factors(nc.sync, sa, "sa_first", 0, 1)
        tl_p.append(load_plane(tl, LAST, "tl"))
        sa_f = sa_f + load_factors(nc.sync, sa, "sa_rest", 1, PLANES)
        wb_codes = sb.tile([P, N], U32, name="wb_codes", align_bytes=64)
        nc.sync.dma_start(wb_codes[:].bitcast(I32), wb_words[0].rearrange("p n t -> p (n t)").bitcast(I32))
        load_scale_rows(wb_scale, wb_scales)
        wo_codes = sb.tile([P, 2 * N], U8, name="wo_codes", align_bytes=64)
        nc.sync.dma_start(wo_codes[:].bitcast(I32), wo_words[0].bitcast(I32))
        load_scale_rows(wo_scale, wo_scales)
        list6 = load_list(offs6, "list6")
        list7 = load_list(offs7, "list7")
        so_f = load_output_factors(so, "so_f")
        sp_f = load_output_factors(sp, "sp_f")

        code = sb.tile([P, PLANES, J], F32, name="code")
        gain = sb.tile([P, PLANES, J], F32, name="gain")
        xc = sb.tile([P, PLANES, J], BF16, name="xc")
        for t in range(PLANES):
            fetch(code[:, t, :], ta_p[t], list1, ga_f[t])
            fetch(gain[:, t, :], tb_p[t], list2, gb_f[t])
            nc.vector.tensor_tensor(xc[:, t, :], code[:, t, :], gain[:, t, :], ALU.mult)
        xc_woven = sb.tile([P, J, PLANES], BF16, name="xc_woven", align_bytes=64)
        nc.vector.tensor_copy(
            xc_woven[:].rearrange("p (c i) t -> p c t i", i=4), xc[:].rearrange("p t (c i) -> p c t i", i=4)
        )
        xc_codes = sb.tile([P, J], U32, name="xc_codes", align_bytes=64)
        xc_scale = sb.tile([P, J], U8, name="xc_scale", align_bytes=64)
        quantize(xc_codes[:], xc_scale[:], xc_woven[:])

        wc = sb.tile([P, PLANES, R], BF16, name="wc")
        wc_woven = sb.tile([P, PLANES, P, PLANES], BF16, name="wc_woven", align_bytes=64)
        wc_codes = sb.tile([P, R], U32, name="wc_codes", align_bytes=64)
        wc_scale = sb.tile([P, R], U8, name="wc_scale", align_bytes=64)

        def weave_wc(t, m, s):
            src = wc[:, t, :].rearrange("p t (m s) -> p s m t", s=PLANES)[:, s, m, :]
            nc.vector.tensor_copy(
                wc_woven[:, s, m, t].rearrange("p s (i e) t -> p i s e t", e=2),
                src.rearrange("p s (i e) t -> p i s e t", e=2),
            )

        low_planes, high_planes = halves(PLANES)
        low_m, high_m = halves(P)
        low_r, high_r = halves(R)
        all_groups = slice(0, PLANES)
        for t in range(low_planes.stop):
            fetch(wc[:, t, :], ua_p[t], list3, ha_f[t])
        weave_wc(low_planes, slice(0, P), all_groups)
        fetch(wc[:, LAST - 1, :], ua_p[LAST - 1], list3, ha_f[LAST - 1])
        fetch(wc[:, LAST, low_r], ua_p[LAST], list3, ha_f[LAST], low_r)
        weave_wc(high_planes, low_m, all_groups)
        fetch(wc[:, LAST, high_r], ua_p[LAST], list3, ha_f[LAST], high_r)
        for s in range(PLANES):
            weave_wc(high_planes, high_m, slice(s, s + 1))
            cols = slice(s * P, (s + 1) * P)
            quantize(wc_codes[:, cols], wc_scale[:, cols], wc_woven[:, s, :, :])

        level = sb.tile([P, PLANES, O], F32, name="level")
        hid_codes = sb.tile([P, O], U32, name="hid_codes", align_bytes=64)
        hid_scale = sb.tile([P, O], U8, name="hid_scale", align_bytes=64)
        p_b = [sb.tile([P, O], F32, name=f"p{c}") for c in range(BLOCKS)]
        q_b = [sb.tile([P, O], F32, name=f"q{c}") for c in range(BLOCKS)]
        a_p = []
        for s in range(PLANES):
            a_p.append(sb.tile([P, J], F32, name=f"a{s}"))
            cols = slice(s * P, (s + 1) * P)
            width = J // 4 if s == 0 else J // 2
            for j0 in range(0, J, width):
                j = slice(j0, j0 + width)
                acc = product(wc_codes[:, cols].bitcast(FP8X4), wc_scale[:, cols], xc_codes[:, j], xc_scale[:, j])
                nc.vector.tensor_copy(a_p[s][:, j], acc[:])

        hidden = sb.tile([P, PLANES, O], F32, name="hidden")

        def outcomes(o):
            hid_woven = sb.tile([P, O // 2, PLANES], BF16, name="hid_woven", tag="hid_woven", align_bytes=64)
            for piece in halves(O // 2):
                nc.vector.tensor_tensor(
                    hid_woven[:, piece, :].rearrange("p (c e) t -> p c t e", e=2),
                    hidden[:, :, o][:, :, piece].rearrange("p t (c e) -> p c t e", e=2),
                    level[:, :, o][:, :, piece].rearrange("p t (c e) -> p c t e", e=2),
                    ALU.max,
                )
            for piece in halves(O // 2):
                quantize(hid_codes[:, o][:, piece], hid_scale[:, o][:, piece], hid_woven[:, piece, :])
            banks = []
            for c in range(BLOCKS):
                cols = slice(c * P, (c + 1) * P)
                wb_block = wb_codes[:, cols].bitcast(FP8X4)
                wo_block = wo_codes[:, 2 * c * P : 2 * (c + 1) * P].bitcast(FP4X4)
                banks.append((p_b[c][:, o], product(wb_block, wb_scale[:, cols], hid_codes[:, o], hid_scale[:, o])))
                banks.append((q_b[c][:, o], product(wo_block, wo_scale[:, cols], hid_codes[:, o], hid_scale[:, o])))
            return banks

        low_o, high_o = halves(O)
        for s in range(PLANES):
            fetch(level[:, s, :], tl_p[s], list5, sl_f[s])
        fetch(hidden[:, 0, :], a_p[0], list4, sa_f[0])
        for s in range(1, PLANES):
            fetch(hidden[:, s, low_o], a_p[s], list4, sa_f[s], low_o)
        banks = outcomes(low_o)
        for s in range(1, PLANES):
            fetch(hidden[:, s, high_o], a_p[s], list4, sa_f[s], high_o)
        for dst, acc in banks + outcomes(high_o):
            nc.vector.tensor_copy(dst, acc[:])

        for c in range(BLOCKS):
            first = sb.tile([P, E], F32, name=f"first{c}")
            second = sb.tile([P, E], F32, name=f"second{c}")
            y = sb.tile([P, E], F32, name=f"y{c}")
            fetch(first[:], p_b[c], list6, so_f[c])
            fetch(second[:], q_b[c], list7, sp_f[c])
            nc.vector.tensor_tensor(y[:], first[:], second[:], ALU.subtract)
            nc.sync.dma_start(out[c * P : (c + 1) * P, :], y[:])
